import numpy as np
import ml_dtypes


def mxq(x, axis, fmt="e4m3"):
    dtype, down = {"e4m3": (ml_dtypes.float8_e4m3fn, 7), "e5m2": (ml_dtypes.float8_e5m2, 14)}[fmt]
    v = np.moveaxis(np.asarray(x, np.float32).astype(ml_dtypes.bfloat16).astype(np.float64), axis, -1)
    blocks = v.reshape(v.shape[:-1] + (-1, 32))
    amax = np.abs(blocks).max(-1, keepdims=True)
    byte = np.maximum(np.where(amax > 0, np.frexp(amax)[1] - 1 + 127, 0) - down, 1)
    scale = np.exp2(byte - 127.0)
    codes = (blocks / scale).astype(np.float32).astype(dtype).astype(np.float64)
    return np.moveaxis((codes * scale).reshape(v.shape), -1, axis)


WIDE = False


def mx_kscale(k):
    if not WIDE:
        return np.ones(k)
    levels = np.array([10, -10, 5, -5, 0])
    if k % 512:
        return np.exp2(np.random.permutation(np.resize(levels, k // 32))).repeat(32)
    a = np.empty((k // 512, 16))
    for p in range(k // 512):
        a[p, :8] = np.random.permutation(np.resize(levels, 8))
        for g in range(8):
            far = levels[np.abs(levels - a[p, g]) >= 10]
            a[p, g + 8] = far[np.random.randint(len(far))]
    return np.exp2(a.ravel()).repeat(32)


def f64(x):
    return np.asarray(x).astype(np.float64)


def striped(idx):
    return np.tile(idx.reshape(-1, 16).T, (8, 1)).astype(np.uint16)


def unstriped(offs):
    return offs[:16].T.reshape(-1).astype(np.int64)


def striped8(idx):
    return np.concatenate([x.reshape(-1, 16).T for x in idx]).astype(np.uint16)


def runs(offs, k):
    lists = np.stack([offs[16 * r : 16 * r + 16].T.reshape(-1) for r in range(8)]).astype(np.int64)
    return lists[np.arange(k) % 512 // 64]


def pack_weight(w):
    k, n = w.shape
    w = f64(np.asarray(w, np.float32).astype(ml_dtypes.bfloat16)).reshape(k // 32, 32, n)
    amax = np.abs(w).max(1)
    byte = np.clip(np.where(amax > 0, np.frexp(amax)[1] - 1 + 127 - 7, 1), 1, 254)
    scaled = (w * np.exp2(127.0 - byte)[:, None, :]).reshape(k, n).astype(np.float32)
    words = np.ascontiguousarray(scaled.reshape(k // 512, 128, 4, n).transpose(0, 1, 3, 2)).astype(ml_dtypes.float8_e4m3fn).view(np.uint8)
    return words, np.ascontiguousarray(byte.astype(np.uint8).reshape(k // 512, 16, n))


def unpack_weight(words, scales):
    g, p, n, _ = words.shape
    vals = np.ascontiguousarray(words).view(ml_dtypes.float8_e4m3fn).astype(np.float64) * np.repeat(np.exp2(scales.astype(np.float64) - 127.0), 8, axis=1)[..., None]
    return vals.transpose(0, 1, 3, 2).reshape(g * 512, n)


def sigmoid(v):
    return 1.0 / (1.0 + np.exp(-np.maximum(v, -700.0)))

def planes(y):
    n, m = y.shape
    v = y.astype(np.float32).astype(ml_dtypes.bfloat16).astype(np.float64).reshape(n // 32, 32, m)
    top = np.abs(v).max(1)
    byte = np.clip(np.where(top > 0, np.frexp(top)[1] - 1 + 127 - 7, 1), 1, 254)
    codes = (v * np.exp2(127.0 - byte)[:, None, :]).reshape(n, m).astype(np.float32).astype(ml_dtypes.float8_e4m3fn).view(np.uint8)
    words = codes.reshape(n // 512, 128, 4, m).transpose(0, 1, 3, 2)
    return np.ascontiguousarray(words), np.ascontiguousarray(byte.astype(np.uint8).reshape(n // 512, 16, m))


K, T, S, N, H, W = 512, 2048, 512, 512, 512, 1024


def setup_inputs():
    n = np.random.standard_normal
    s = mx_kscale(K)[:, None]
    u = mx_kscale(S)
    packed_xT = pack_weight(n((K, T)) * s)
    packed_w1 = pack_weight(n((S, N)) / np.sqrt(S) / u[:, None])
    return {
        "x_words": packed_xT[0],
        "x_scales": packed_xT[1],
        "wa": (n((K, H)) / np.sqrt(K) / s).astype(np.float32),
        "tau": np.random.uniform(0.2, 0.6, (S, 1)).astype(np.float32),
        "tau2": np.random.uniform(0.6, 1.0, (S, 1)).astype(np.float32),
        "gt": (np.random.uniform(0.5, 1.5, (S, 1)) * u[:, None]).astype(np.float32),
        "w1_words": packed_w1[0],
        "w1_scales": packed_w1[1],
        "offs": striped(np.random.permutation(T)[:S]),
        "n1": striped8(np.stack([np.random.permutation(H) for _ in range(8)])),
        "n2": striped8(np.stack([np.random.permutation(H) for _ in range(8)])),
        "n3": striped(np.random.randint(0, H, W)),
    }


def reference(x_words, x_scales, wa, tau, tau2, gt, w1_words, w1_scales, offs, n1, n2, n3):
    xq = unpack_weight(x_words, x_scales)[:, unstriped(offs)]
    y = xq.T @ mxq(f64(wa), 0, "e4m3")
    top = y.max(axis=1, keepdims=True)
    ea = np.exp(f64(tau) * (y[np.arange(S)[:, None], runs(n1, S)] - top))
    ea2 = np.exp(f64(tau2) * (y[np.arange(S)[:, None], runs(n2, S)] - top))
    z = f64(gt) * (3.0 * (ea - ea2))
    h = unpack_weight(w1_words, w1_scales).T @ mxq(z, 0, "e4m3")
    mb = h[:, unstriped(n3)]
    mn = mb.reshape(N, H, 2).min(axis=2)
    mx = mb.reshape(N, H, 2).max(axis=2)
    out_0 = (h - mn) * sigmoid(mx)
    return (out_0,) + planes(out_0)

@@ -1,0 +1,199 @@
+from contextlib import ExitStack
+
+import concourse.mybir as mybir
+
+K, T, S, N, H = 512, 2048, 512, 512, 512
+FLOPS = 2 * K * S * H + 2 * S * N * H
+
+F32 = mybir.dt.float32
+BF16 = mybir.dt.bfloat16
+I32 = mybir.dt.int32
+U32 = mybir.dt.uint32
+U16 = mybir.dt.uint16
+U8 = mybir.dt.uint8
+FP8X4 = mybir.dt.float8_e4m3fn_x4
+ALU = mybir.AluOpType
+ACT = mybir.ActivationFunctionType
+
+P = 128
+PACK = 4
+LIST_ROWS = 16
+SPARE = 16
+WA_HALF = H // 2
+WA_SCALAR_COLS = 96
+Z_CHUNKS = [(0, 256), (256, 128), (384, 128)]
+OUT_CHUNKS = [(0, 256), (256, 256)]
+
+
+def weave_out(grouped):
+    return grouped.rearrange("p (c i) t -> p c t i", i=4)
+
+
+def weave_in(rows):
+    return rows.rearrange("p t (c i) -> p c t i", i=4)
+
+
+def tile_picked_toketwghard_none_po_kernel(
+    tc, x_words, x_scales, wa, tau, tau2, gt, w1_words, w1_scales, offs, n1, n2, n3, out_0, out_1, out_2
+):
+    nc = tc.nc
+    with ExitStack() as ctx:
+        keep = ctx.enter_context(tc.tile_pool(name="keep", bufs=1))
+        psum = ctx.enter_context(tc.psum_pool(name="psum", bufs=1))
+
+        def sb(shape, dtype, name):
+            return keep.tile(shape, dtype, name=name, align_bytes=64)
+
+        offs_sb = sb([P, S // LIST_ROWS], U16, "offs_sb")
+        n1_sb = sb([P, H // LIST_ROWS], U16, "n1_sb")
+        n2_sb = sb([P, H // LIST_ROWS], U16, "n2_sb")
+        n3_sb = sb([P, 2 * H // LIST_ROWS], U16, "n3_sb")
+
+        xw = sb([P, T], I32, "xw")
+        xs = sb([P, T], U8, "xs")
+        w1w = sb([P, N], I32, "w1w")
+        w1s = sb([P, N], U8, "w1s")
+        wa_raw = [sb([P, PACK, WA_HALF], F32, "wa_raw%d" % a) for a in range(2)]
+        rates = sb([P, 3, 8], F32, "rates")
+        hh = [sb([P, H + SPARE], F32, "hh%d" % t) for t in range(PACK)]
+
+        nc.vector.memset(xs[:].bitcast(I32), 0)
+        nc.sync.dma_start(offs_sb[:], offs)
+        nc.sync.dma_start(xw[:], x_words[0].rearrange("p n t -> p (n t)").bitcast(I32))
+        for q in range(4):
+            nc.scalar.dma_start(xs[32 * q : 32 * q + 4, :].bitcast(I32), x_scales[0][4 * q : 4 * q + 4, :].bitcast(I32))
+        wa_rows = wa.rearrange("(p j) h -> p j h", j=PACK)
+        for a in range(2):
+            nc.sync.dma_start(wa_raw[a][:], wa_rows[:, :, a * WA_HALF : (a + 1) * WA_HALF])
+        nc.sync.dma_start(n1_sb[:], n1)
+        nc.sync.dma_start(n2_sb[:], n2)
+        for r, vec in enumerate((tau, tau2, gt)):
+            nc.sync.dma_start(rates[:, r, 0:PACK], vec.rearrange("(p t) o -> p (t o)", t=PACK))
+        nc.vector.memset(w1s[:].bitcast(I32), 0)
+        for t in range(PACK):
+            nc.vector.memset(hh[t][:, H:], 0.0)
+        nc.sync.dma_start(w1w[:], w1_words[0].rearrange("p n t -> p (n t)").bitcast(I32))
+        for q in range(4):
+            nc.sync.dma_start(w1s[32 * q : 32 * q + 4, :].bitcast(I32), w1_scales[0][4 * q : 4 * q + 4, :].bitcast(I32))
+        nc.sync.dma_start(n3_sb[:], n3)
+
+        xgs = sb([P, PACK, P], U8, "xgs")
+        xgw = sb([P, PACK, P], U32, "xgw")
+        nc.vector.tensor_copy(xgs[:].rearrange("p t m -> p m t"), xs[:].indirect(offs_sb[:]))
+        nc.vector.tensor_copy(xgw[:].rearrange("p t m -> p m t"), xw[:].bitcast(U32).indirect(offs_sb[:]))
+
+        wa_codes = sb([P, H], U32, "wa_codes")
+        wa_scales = sb([P, H], U8, "wa_scales")
+        wa_bf = [sb([P, WA_HALF, PACK], BF16, "wa_bf%d" % a) for a in range(2)]
+        nc.scalar.activation(weave_out(wa_bf[0][:]), weave_in(wa_raw[0][:]), ACT.Copy)
+        nc.scalar.activation(weave_out(wa_bf[1][:, :WA_SCALAR_COLS, :]), weave_in(wa_raw[1][:, :, :WA_SCALAR_COLS]), ACT.Copy)
+        nc.vector.tensor_copy(weave_out(wa_bf[1][:, WA_SCALAR_COLS:, :]), weave_in(wa_raw[1][:, :, WA_SCALAR_COLS:]))
+        for a in range(2):
+            cols = slice(a * WA_HALF, (a + 1) * WA_HALF)
+            nc.vector.quantize_mx(
+                out=wa_codes[:, cols].bitcast(FP8X4), scales=wa_scales[:, cols], in_=wa_bf[a][:].rearrange("p w t -> p (w t)")
+            )
+
+        gain = sb([P, PACK], F32, "gain")
+        nc.vector.tensor_scalar(gain[:], rates[:, 2, 0:PACK], 3.0, None, ALU.mult)
+
+        y = [sb([P, H], F32, "y%d" % t) for t in range(PACK)]
+        top = [sb([P, 1], F32, "top%d" % t) for t in range(PACK)]
+        bias = [sb([P, 2], F32, "bias%d" % t) for t in range(PACK)]
+        for t in range(PACK):
+            y_ps = psum.tile([P, H], F32, name="y_ps%d" % t, tag="first%d" % t)
+            nc.tensor.matmul_mx(
+                out=y_ps[:], lhsT=xgw[:, t, :].bitcast(FP8X4), lhsT_scale=xgs[:, t, :],
+                rhs=wa_codes[:].bitcast(FP8X4), rhs_scale=wa_scales[:], start=True, stop=True,
+            )
+            nc.vector.tensor_scalar(y[t][:], y_ps[:], 1.0, None, ALU.mult, ALU.max, accum_out=top[t][:])
+            nc.vector.tensor_scalar(bias[t][:], rates[:, 0:2, t], top[t][:], -1.0, ALU.mult, ALU.mult)
+
+        w1w_d = sb([P, PACK, P], I32, "w1w_d")
+        w1s_d = sb([P, PACK, P], U8, "w1s_d")
+
+        def deal_w1():
+            nc.vector.tensor_copy(w1w_d[:].rearrange("p t m -> p m t"), w1w[:].rearrange("p (m t) -> p m t", t=PACK))
+            nc.vector.tensor_copy(w1s_d[:].rearrange("p t m -> p m t"), w1s[:].rearrange("p (m t) -> p m t", t=PACK))
+
+        early = H - Z_CHUNKS[-1][1]
+        h_early = [psum.tile([P, early], F32, name="h_early%d" % t) for t in range(PACK)]
+        h_last = []
+        for c, (c0, w) in enumerate(Z_CHUNKS):
+            entries = slice(c0 // LIST_ROWS, (c0 + w) // LIST_ROWS)
+            diff = sb([P, PACK, w], F32, "diff%d" % c)
+            for t in range(PACK):
+                ea = sb([P, w], F32, "ea%d_%d" % (c, t))
+                eb = sb([P, w], F32, "eb%d_%d" % (c, t))
+                nc.scalar.activation(ea[:], y[t][:].indirect(n1_sb[:, entries]), ACT.Exp, bias=bias[t][:, 0:1], scale=rates[:, 0, t : t + 1])
+                nc.scalar.activation(eb[:], y[t][:].indirect(n2_sb[:, entries]), ACT.Exp, bias=bias[t][:, 1:2], scale=rates[:, 1, t : t + 1])
+                nc.vector.tensor_tensor(diff[:, t, :], ea[:], eb[:], ALU.subtract)
+            z_bf = sb([P, w, PACK], BF16, "z_bf%d" % c)
+            nc.vector.tensor_tensor(
+                weave_out(z_bf[:]), weave_in(diff[:]), gain[:].unsqueeze(1).unsqueeze(3).to_broadcast([P, w // 4, PACK, 4]), ALU.mult
+            )
+            z_codes = sb([P, w], U32, "z_codes%d" % c)
+            z_scales = sb([P, w], U8, "z_scales%d" % c)
+            if c == 0:
+                deal_w1()
+            nc.vector.quantize_mx(out=z_codes[:].bitcast(FP8X4), scales=z_scales[:], in_=z_bf[:].rearrange("p w t -> p (w t)"))
+            for t in range(PACK):
+                if c0 < early:
+                    h_ps = h_early[t][:, c0 : c0 + w]
+                else:
+                    bank = psum.tile([P, H], F32, name="h_last%d" % t, tag="first%d" % t)
+                    h_ps = bank[:, :w]
+                    h_last.append(h_ps)
+                nc.tensor.matmul_mx(
+                    out=h_ps, lhsT=w1w_d[:, t, :].bitcast(FP8X4), lhsT_scale=w1s_d[:, t, :],
+                    rhs=z_codes[:].bitcast(FP8X4), rhs_scale=z_scales[:], start=True, stop=True,
+                )
+
+        for t in range(PACK):
+            nc.scalar.activation(hh[t][:, :early], h_early[t][:], ACT.Copy, scale=0.5)
+        for t in range(PACK):
+            if t % 2 == 0:
+                nc.vector.tensor_scalar(hh[t][:, early:H], h_last[t], 0.5, None, ALU.mult)
+            else:
+                nc.scalar.activation(hh[t][:, early:H], h_last[t], ACT.Copy, scale=0.5)
+
+        out_rows = out_0.rearrange("(p t) j -> p t j", t=PACK)
+        out_words = out_1[0].rearrange("p n t -> p (n t)").bitcast(I32)
+        o_codes = sb([P, H], U32, "o_codes")
+        o_scales = sb([P, H], U8, "o_scales")
+        res = []
+        for c, (c0, w) in enumerate(OUT_CHUNKS):
+            entries = slice(2 * c0 // LIST_ROWS, 2 * (c0 + w) // LIST_ROWS)
+            o = sb([P, PACK, w], F32, "o%d" % c)
+            res.append(o)
+            for t in range(PACK):
+                pair = sb([P, w, 2], F32, "pair%d_%d" % (c, t))
+                picked = hh[t][:].indirect(n3_sb[:, entries])
+                flat = pair[:].rearrange("p j e -> p (j e)")
+                if c == 0 and t == 0:
+                    nc.vector.tensor_copy(flat, picked)
+                else:
+                    nc.scalar.activation(flat, picked, ACT.Copy)
+                big = sb([P, w], F32, "big%d_%d" % (c, t))
+                small = sb([P, w], F32, "small%d_%d" % (c, t))
+                th = sb([P, w], F32, "th%d_%d" % (c, t))
+                rest = sb([P, w], F32, "rest%d_%d" % (c, t))
+                nc.vector.tensor_tensor(big[:], pair[:, :, 0], pair[:, :, 1], ALU.max)
+                nc.vector.tensor_tensor(small[:], pair[:, :, 0], pair[:, :, 1], ALU.min)
+                nc.scalar.activation(th[:], big[:], ACT.Tanh)
+                nc.vector.tensor_tensor(rest[:], hh[t][:, c0 : c0 + w], small[:], ALU.subtract)
+                nc.vector.scalar_tensor_tensor(o[:, t, :], th[:], 1.0, rest[:], ALU.add, ALU.mult)
+                if t % 2 == 1:
+                    nc.sync.dma_start(out_rows[:, t - 1 : t + 1, c0 : c0 + w], o[:, t - 1 : t + 1, :])
+        for c, (c0, w) in enumerate(OUT_CHUNKS):
+            o_bf = sb([P, w, PACK], BF16, "o_bf%d" % c)
+            if c == 0:
+                nc.scalar.activation(weave_out(o_bf[:]), weave_in(res[c][:]), ACT.Copy)
+            else:
+                nc.vector.tensor_copy(weave_out(o_bf[:]), weave_in(res[c][:]))
+            cols = slice(c0, c0 + w)
+            nc.vector.quantize_mx(out=o_codes[:, cols].bitcast(FP8X4), scales=o_scales[:, cols], in_=o_bf[:].rearrange("p w t -> p (w t)"))
+            nc.sync.dma_start(out_words[:, cols], o_codes[:, cols].bitcast(I32))
+        for q in range(4):
+            eng = nc.scalar if q % 2 == 0 else nc.sync
+            eng.dma_start(out_2[0][4 * q : 4 * q + 4, :].bitcast(I32), o_scales[32 * q : 32 * q + 4, :].bitcast(I32))

@@ -19,10 +19,11 @@ P = 128
 PACK = 4
 LIST_ROWS = 16
 SPARE = 16
-WA_HALF = H // 2
-WA_SCALAR_COLS = 96
+WA_PIECES = [(0, 256), (256, 128), (384, 128)]
+HALF = H // 2
+RING = 3
 Z_CHUNKS = [(0, 256), (256, 128), (384, 128)]
-OUT_CHUNKS = [(0, 256), (256, 256)]
+OUT_CHUNKS = [(0, 256), (256, 128), (384, 128)]
 
 
 def weave_out(grouped):
@@ -53,26 +54,27 @@ def tile_picked_toketwghard_none_po_kernel(
         xs = sb([P, T], U8, "xs")
         w1w = sb([P, N], I32, "w1w")
         w1s = sb([P, N], U8, "w1s")
-        wa_raw = [sb([P, PACK, WA_HALF], F32, "wa_raw%d" % a) for a in range(2)]
+        wa_raw = [sb([P, PACK, w], F32, "wa_raw%d" % a) for a, (c0, w) in enumerate(WA_PIECES)]
         rates = sb([P, 3, 8], F32, "rates")
         hh = [sb([P, H + SPARE], F32, "hh%d" % t) for t in range(PACK)]
 
-        nc.vector.memset(xs[:].bitcast(I32), 0)
+        nc.gpsimd.memset(xs[:].bitcast(I32), 0)
         nc.sync.dma_start(offs_sb[:], offs)
         nc.sync.dma_start(xw[:], x_words[0].rearrange("p n t -> p (n t)").bitcast(I32))
         for q in range(4):
             nc.scalar.dma_start(xs[32 * q : 32 * q + 4, :].bitcast(I32), x_scales[0][4 * q : 4 * q + 4, :].bitcast(I32))
         wa_rows = wa.rearrange("(p j) h -> p j h", j=PACK)
-        for a in range(2):
-            nc.sync.dma_start(wa_raw[a][:], wa_rows[:, :, a * WA_HALF : (a + 1) * WA_HALF])
-        nc.sync.dma_start(n1_sb[:], n1)
-        nc.sync.dma_start(n2_sb[:], n2)
-        for r, vec in enumerate((tau, tau2, gt)):
-            nc.sync.dma_start(rates[:, r, 0:PACK], vec.rearrange("(p t) o -> p (t o)", t=PACK))
-        nc.vector.memset(w1s[:].bitcast(I32), 0)
+        for a, (c0, w) in enumerate(WA_PIECES):
+            nc.sync.dma_start(wa_raw[a][:], wa_rows[:, :, c0 : c0 + w])
+        nc.gpsimd.memset(w1s[:].bitcast(I32), 0)
         for t in range(PACK):
-            nc.vector.memset(hh[t][:, H:], 0.0)
+            nc.gpsimd.memset(hh[t][:, H:], 0.0)
+        nc.sync.dma_start(n2_sb[:], n2)
+        nc.sync.dma_start(n1_sb[:], n1)
+        for r, vec in enumerate((tau, tau2)):
+            nc.sync.dma_start(rates[:, r, 0:PACK], vec.rearrange("(p t) o -> p (t o)", t=PACK))
         nc.sync.dma_start(w1w[:], w1_words[0].rearrange("p n t -> p (n t)").bitcast(I32))
+        nc.sync.dma_start(rates[:, 2, 0:PACK], gt.rearrange("(p t) o -> p (t o)", t=PACK))
         for q in range(4):
             nc.sync.dma_start(w1s[32 * q : 32 * q + 4, :].bitcast(I32), w1_scales[0][4 * q : 4 * q + 4, :].bitcast(I32))
         nc.sync.dma_start(n3_sb[:], n3)
@@ -84,64 +86,68 @@ def tile_picked_toketwghard_none_po_kernel(
 
         wa_codes = sb([P, H], U32, "wa_codes")
         wa_scales = sb([P, H], U8, "wa_scales")
-        wa_bf = [sb([P, WA_HALF, PACK], BF16, "wa_bf%d" % a) for a in range(2)]
-        nc.scalar.activation(weave_out(wa_bf[0][:]), weave_in(wa_raw[0][:]), ACT.Copy)
-        nc.scalar.activation(weave_out(wa_bf[1][:, :WA_SCALAR_COLS, :]), weave_in(wa_raw[1][:, :, :WA_SCALAR_COLS]), ACT.Copy)
-        nc.vector.tensor_copy(weave_out(wa_bf[1][:, WA_SCALAR_COLS:, :]), weave_in(wa_raw[1][:, :, WA_SCALAR_COLS:]))
-        for a in range(2):
-            cols = slice(a * WA_HALF, (a + 1) * WA_HALF)
+        for a, (c0, w) in enumerate(WA_PIECES):
+            wa_bf = sb([P, w, PACK], BF16, "wa_bf%d" % a)
+            if a == 0:
+                nc.scalar.activation(weave_out(wa_bf[:]), weave_in(wa_raw[a][:]), ACT.Copy)
+            else:
+                nc.vector.tensor_copy(weave_out(wa_bf[:]), weave_in(wa_raw[a][:]))
             nc.vector.quantize_mx(
-                out=wa_codes[:, cols].bitcast(FP8X4), scales=wa_scales[:, cols], in_=wa_bf[a][:].rearrange("p w t -> p (w t)")
+                out=wa_codes[:, c0 : c0 + w].bitcast(FP8X4), scales=wa_scales[:, c0 : c0 + w], in_=wa_bf[:].rearrange("p w t -> p (w t)")
             )
+
+        y = [sb([P, H], F32, "y%d" % t) for t in range(PACK)]
+        top = [sb([P, 2], F32, "top%d" % t) for t in range(PACK)]
+        bias = [sb([P, 2], F32, "bias%d" % t) for t in range(PACK)]
+        y_ps = {}
+        for half in range(2):
+            cols = slice(half * HALF, (half + 1) * HALF)
+            for t in range(PACK):
+                bank = psum.tile([P, H], F32, name="y_ps%d_%d" % (half, t), tag="bank%d_%d" % (half, t))
+                y_ps[half, t] = bank
+                nc.tensor.matmul_mx(
+                    out=bank[:, :HALF], lhsT=xgw[:, t, :].bitcast(FP8X4), lhsT_scale=xgs[:, t, :],
+                    rhs=wa_codes[:, cols].bitcast(FP8X4), rhs_scale=wa_scales[:, cols], start=True, stop=True,
+                )
+        for t in range(PACK):
+            nc.vector.tensor_scalar(y[t][:, :HALF], y_ps[0, t][:, :HALF], 1.0, None, ALU.mult, ALU.max, accum_out=top[t][:, 0:1])
+            nc.vector.tensor_scalar(y[t][:, HALF:], y_ps[1, t][:, :HALF], 1.0, top[t][:, 0:1], ALU.mult, ALU.max, accum_out=top[t][:, 1:2])
+            nc.vector.tensor_scalar(bias[t][:], rates[:, 0:2, t], top[t][:, 1:2], -1.0, ALU.mult, ALU.mult)
 
         gain = sb([P, PACK], F32, "gain")
         nc.vector.tensor_scalar(gain[:], rates[:, 2, 0:PACK], 3.0, None, ALU.mult)
 
-        y = [sb([P, H], F32, "y%d" % t) for t in range(PACK)]
-        top = [sb([P, 1], F32, "top%d" % t) for t in range(PACK)]
-        bias = [sb([P, 2], F32, "bias%d" % t) for t in range(PACK)]
-        for t in range(PACK):
-            y_ps = psum.tile([P, H], F32, name="y_ps%d" % t, tag="first%d" % t)
-            nc.tensor.matmul_mx(
-                out=y_ps[:], lhsT=xgw[:, t, :].bitcast(FP8X4), lhsT_scale=xgs[:, t, :],
-                rhs=wa_codes[:].bitcast(FP8X4), rhs_scale=wa_scales[:], start=True, stop=True,
-            )
-            nc.vector.tensor_scalar(y[t][:], y_ps[:], 1.0, None, ALU.mult, ALU.max, accum_out=top[t][:])
-            nc.vector.tensor_scalar(bias[t][:], rates[:, 0:2, t], top[t][:], -1.0, ALU.mult, ALU.mult)
-
-        w1w_d = sb([P, PACK, P], I32, "w1w_d")
+        w1w_d = sb([P, PACK, P], U32, "w1w_d")
         w1s_d = sb([P, PACK, P], U8, "w1s_d")
+        nc.scalar.copy(w1w_d[:], w1w[:].bitcast(U32).rearrange("p (m t) -> p t m", t=PACK))
+        nc.vector.tensor_copy(w1s_d[:].rearrange("p t m -> p m t"), w1s[:].rearrange("p (m t) -> p m t", t=PACK))
 
-        def deal_w1():
-            nc.vector.tensor_copy(w1w_d[:].rearrange("p t m -> p m t"), w1w[:].rearrange("p (m t) -> p m t", t=PACK))
-            nc.vector.tensor_copy(w1s_d[:].rearrange("p t m -> p m t"), w1s[:].rearrange("p (m t) -> p m t", t=PACK))
-
+        ea_ring = [sb([P, HALF], F32, "ea%d" % i) for i in range(RING)]
+        eb_ring = [sb([P, HALF], F32, "eb%d" % i) for i in range(RING)]
         early = H - Z_CHUNKS[-1][1]
-        h_early = [psum.tile([P, early], F32, name="h_early%d" % t) for t in range(PACK)]
+        h_early = [psum.tile([P, H], F32, name="h_early%d" % t, tag="bank0_%d" % t) for t in range(PACK)]
         h_last = []
         for c, (c0, w) in enumerate(Z_CHUNKS):
             entries = slice(c0 // LIST_ROWS, (c0 + w) // LIST_ROWS)
             diff = sb([P, PACK, w], F32, "diff%d" % c)
             for t in range(PACK):
-                ea = sb([P, w], F32, "ea%d_%d" % (c, t))
-                eb = sb([P, w], F32, "eb%d_%d" % (c, t))
-                nc.scalar.activation(ea[:], y[t][:].indirect(n1_sb[:, entries]), ACT.Exp, bias=bias[t][:, 0:1], scale=rates[:, 0, t : t + 1])
-                nc.scalar.activation(eb[:], y[t][:].indirect(n2_sb[:, entries]), ACT.Exp, bias=bias[t][:, 1:2], scale=rates[:, 1, t : t + 1])
-                nc.vector.tensor_tensor(diff[:, t, :], ea[:], eb[:], ALU.subtract)
+                ea = ea_ring[(c * PACK + t) % RING][:, :w]
+                eb = eb_ring[(c * PACK + t) % RING][:, :w]
+                ebg = sb([P, w], F32, "ebg%d_%d" % (c, t))
+                nc.scalar.activation(eb, y[t][:].indirect(n2_sb[:, entries]), ACT.Exp, bias=bias[t][:, 1:2], scale=rates[:, 1, t : t + 1])
+                nc.scalar.activation(ea, y[t][:].indirect(n1_sb[:, entries]), ACT.Exp, bias=bias[t][:, 0:1], scale=rates[:, 0, t : t + 1])
+                nc.vector.tensor_scalar(ebg[:], eb, gain[:, t : t + 1], None, ALU.mult)
+                nc.vector.scalar_tensor_tensor(diff[:, t, :], ea, gain[:, t : t + 1], ebg[:], ALU.mult, ALU.subtract)
             z_bf = sb([P, w, PACK], BF16, "z_bf%d" % c)
-            nc.vector.tensor_tensor(
-                weave_out(z_bf[:]), weave_in(diff[:]), gain[:].unsqueeze(1).unsqueeze(3).to_broadcast([P, w // 4, PACK, 4]), ALU.mult
-            )
+            nc.vector.tensor_copy(weave_out(z_bf[:]), weave_in(diff[:]))
             z_codes = sb([P, w], U32, "z_codes%d" % c)
             z_scales = sb([P, w], U8, "z_scales%d" % c)
-            if c == 0:
-                deal_w1()
             nc.vector.quantize_mx(out=z_codes[:].bitcast(FP8X4), scales=z_scales[:], in_=z_bf[:].rearrange("p w t -> p (w t)"))
             for t in range(PACK):
                 if c0 < early:
                     h_ps = h_early[t][:, c0 : c0 + w]
                 else:
-                    bank = psum.tile([P, H], F32, name="h_last%d" % t, tag="first%d" % t)
+                    bank = psum.tile([P, H], F32, name="h_last%d" % t, tag="bank1_%d" % t)
                     h_ps = bank[:, :w]
                     h_last.append(h_ps)
                 nc.tensor.matmul_mx(
@@ -150,7 +156,7 @@ def tile_picked_toketwghard_none_po_kernel(
                 )
 
         for t in range(PACK):
-            nc.scalar.activation(hh[t][:, :early], h_early[t][:], ACT.Copy, scale=0.5)
+            nc.scalar.activation(hh[t][:, :early], h_early[t][:, :early], ACT.Copy, scale=0.5)
         for t in range(PACK):
             if t % 2 == 0:
                 nc.vector.tensor_scalar(hh[t][:, early:H], h_last[t], 0.5, None, ALU.mult)
@@ -161,39 +167,65 @@ def tile_picked_toketwghard_none_po_kernel(
         out_words = out_1[0].rearrange("p n t -> p (n t)").bitcast(I32)
         o_codes = sb([P, H], U32, "o_codes")
         o_scales = sb([P, H], U8, "o_scales")
-        res = []
-        for c, (c0, w) in enumerate(OUT_CHUNKS):
+        res = [sb([P, PACK, w], F32, "o%d" % c) for c, (c0, w) in enumerate(OUT_CHUNKS)]
+        units = [(c, t) for c in range(len(OUT_CHUNKS)) for t in range(PACK)]
+        held = {}
+        pair_ring = [sb([P, HALF, 2], F32, "pair%d" % i) for i in range(RING)]
+
+        def front(u):
+            c, t = units[u]
+            c0, w = OUT_CHUNKS[c]
             entries = slice(2 * c0 // LIST_ROWS, 2 * (c0 + w) // LIST_ROWS)
-            o = sb([P, PACK, w], F32, "o%d" % c)
-            res.append(o)
-            for t in range(PACK):
-                pair = sb([P, w, 2], F32, "pair%d_%d" % (c, t))
-                picked = hh[t][:].indirect(n3_sb[:, entries])
-                flat = pair[:].rearrange("p j e -> p (j e)")
-                if c == 0 and t == 0:
-                    nc.vector.tensor_copy(flat, picked)
-                else:
-                    nc.scalar.activation(flat, picked, ACT.Copy)
-                big = sb([P, w], F32, "big%d_%d" % (c, t))
-                small = sb([P, w], F32, "small%d_%d" % (c, t))
-                th = sb([P, w], F32, "th%d_%d" % (c, t))
-                rest = sb([P, w], F32, "rest%d_%d" % (c, t))
-                nc.vector.tensor_tensor(big[:], pair[:, :, 0], pair[:, :, 1], ALU.max)
-                nc.vector.tensor_tensor(small[:], pair[:, :, 0], pair[:, :, 1], ALU.min)
-                nc.scalar.activation(th[:], big[:], ACT.Tanh)
-                nc.vector.tensor_tensor(rest[:], hh[t][:, c0 : c0 + w], small[:], ALU.subtract)
-                nc.vector.scalar_tensor_tensor(o[:, t, :], th[:], 1.0, rest[:], ALU.add, ALU.mult)
-                if t % 2 == 1:
-                    nc.sync.dma_start(out_rows[:, t - 1 : t + 1, c0 : c0 + w], o[:, t - 1 : t + 1, :])
-        for c, (c0, w) in enumerate(OUT_CHUNKS):
+            pair = pair_ring[u % RING][:, :w, :]
+            picked = hh[t][:].indirect(n3_sb[:, entries])
+            flat = pair.rearrange("p j e -> p (j e)")
+            if u == 0:
+                nc.vector.tensor_copy(flat, picked)
+            else:
+                nc.scalar.activation(flat, picked, ACT.Copy)
+            big = sb([P, w], F32, "big%d" % u)
+            small = sb([P, w], F32, "small%d" % u)
+            th = sb([P, w], F32, "th%d" % u)
+            nc.vector.tensor_tensor(big[:], pair[:, :, 0], pair[:, :, 1], ALU.max)
+            nc.vector.tensor_tensor(small[:], pair[:, :, 0], pair[:, :, 1], ALU.min)
+            nc.scalar.activation(th[:], big[:], ACT.Tanh)
+            held[u] = (small, th)
+
+        def middle(u):
+            c, t = units[u]
+            c0, w = OUT_CHUNKS[c]
+            small, th = held[u]
+            rest = sb([P, w], F32, "rest%d" % u)
+            nc.vector.tensor_tensor(rest[:], hh[t][:, c0 : c0 + w], small[:], ALU.subtract)
+            held[u] = (rest, th)
+
+        def back(u):
+            c, t = units[u]
+            c0, w = OUT_CHUNKS[c]
+            rest, th = held[u]
+            nc.vector.scalar_tensor_tensor(res[c][:, t, :], th[:], 1.0, rest[:], ALU.add, ALU.mult)
+            if t == PACK - 1:
+                nc.sync.dma_start(out_rows[:, :, c0 : c0 + w], res[c][:])
+
+        def planes(c):
+            c0, w = OUT_CHUNKS[c]
             o_bf = sb([P, w, PACK], BF16, "o_bf%d" % c)
-            if c == 0:
+            if c < len(OUT_CHUNKS) - 1:
                 nc.scalar.activation(weave_out(o_bf[:]), weave_in(res[c][:]), ACT.Copy)
             else:
                 nc.vector.tensor_copy(weave_out(o_bf[:]), weave_in(res[c][:]))
             cols = slice(c0, c0 + w)
             nc.vector.quantize_mx(out=o_codes[:, cols].bitcast(FP8X4), scales=o_scales[:, cols], in_=o_bf[:].rearrange("p w t -> p (w t)"))
             nc.sync.dma_start(out_words[:, cols], o_codes[:, cols].bitcast(I32))
+
+        for u in range(len(units)):
+            front(u)
+            if u > 0:
+                back(u - 1)
+            middle(u)
+        back(len(units) - 1)
+        for c in range(len(OUT_CHUNKS)):
+            planes(c)
         for q in range(4):
             eng = nc.scalar if q % 2 == 0 else nc.sync
             eng.dma_start(out_2[0][4 * q : 4 * q + 4, :].bitcast(I32), o_scales[32 * q : 32 * q + 4, :].bitcast(I32))

@@ -18,12 +18,13 @@ ACT = mybir.ActivationFunctionType
 P = 128
 PACK = 4
 LIST_ROWS = 16
-SPARE = 16
+SPARE = 272
 WA_PIECES = [(0, 256), (256, 128), (384, 128)]
 HALF = H // 2
-RING = 3
+RING = 2
 Z_CHUNKS = [(0, 256), (256, 128), (384, 128)]
-OUT_CHUNKS = [(0, 256), (256, 128), (384, 128)]
+OUT_CHUNKS = [(0, 384), (384, 128)]
+EXP_STEPS = [(0, 0, 512), (1, 0, 256), (2, 0, 256), (3, 0, 256), (1, 256, 256), (2, 256, 256), (3, 256, 128), (3, 384, 128)]
 
 
 def weave_out(grouped):
@@ -42,8 +43,8 @@ def tile_picked_toketwghard_none_po_kernel(
         keep = ctx.enter_context(tc.tile_pool(name="keep", bufs=1))
         psum = ctx.enter_context(tc.psum_pool(name="psum", bufs=1))
 
-        def sb(shape, dtype, name):
-            return keep.tile(shape, dtype, name=name, align_bytes=64)
+        def sb(shape, dtype, name, tag=""):
+            return keep.tile(shape, dtype, name=name, tag=tag or name, align_bytes=64)
 
         offs_sb = sb([P, S // LIST_ROWS], U16, "offs_sb")
         n1_sb = sb([P, H // LIST_ROWS], U16, "n1_sb")
@@ -58,23 +59,28 @@ def tile_picked_toketwghard_none_po_kernel(
         rates = sb([P, 3, 8], F32, "rates")
         hh = [sb([P, H + SPARE], F32, "hh%d" % t) for t in range(PACK)]
 
-        nc.gpsimd.memset(xs[:].bitcast(I32), 0)
-        nc.sync.dma_start(offs_sb[:], offs)
-        nc.sync.dma_start(xw[:], x_words[0].rearrange("p n t -> p (n t)").bitcast(I32))
-        for q in range(4):
-            nc.scalar.dma_start(xs[32 * q : 32 * q + 4, :].bitcast(I32), x_scales[0][4 * q : 4 * q + 4, :].bitcast(I32))
+        nc.vector.memset(xs[:].bitcast(I32), 0)
         wa_rows = wa.rearrange("(p j) h -> p j h", j=PACK)
-        for a, (c0, w) in enumerate(WA_PIECES):
+
+        def load_wa(a):
+            c0, w = WA_PIECES[a]
             nc.sync.dma_start(wa_raw[a][:], wa_rows[:, :, c0 : c0 + w])
-        nc.gpsimd.memset(w1s[:].bitcast(I32), 0)
+
+        nc.sync.dma_start(offs_sb[:], offs)
+        load_wa(0)
+        for q in range(4):
+            nc.sync.dma_start(xs[32 * q : 32 * q + 4, :].bitcast(I32), x_scales[0][4 * q : 4 * q + 4, :].bitcast(I32))
+        nc.sync.dma_start(xw[:], x_words[0].rearrange("p n t -> p (n t)").bitcast(I32))
+        load_wa(1)
+        load_wa(2)
+        nc.vector.memset(w1s[:].bitcast(I32), 0)
         for t in range(PACK):
-            nc.gpsimd.memset(hh[t][:, H:], 0.0)
+            nc.vector.memset(hh[t][:, H:], 0.0)
         nc.sync.dma_start(n2_sb[:], n2)
         nc.sync.dma_start(n1_sb[:], n1)
-        for r, vec in enumerate((tau, tau2)):
-            nc.sync.dma_start(rates[:, r, 0:PACK], vec.rearrange("(p t) o -> p (t o)", t=PACK))
+        for r, vec in enumerate((tau, tau2, gt)):
+            nc.gpsimd.dma_start(rates[:, r, 0:PACK], vec.rearrange("(p t) o -> p (t o)", t=PACK))
         nc.sync.dma_start(w1w[:], w1_words[0].rearrange("p n t -> p (n t)").bitcast(I32))
-        nc.sync.dma_start(rates[:, 2, 0:PACK], gt.rearrange("(p t) o -> p (t o)", t=PACK))
         for q in range(4):
             nc.sync.dma_start(w1s[32 * q : 32 * q + 4, :].bitcast(I32), w1_scales[0][4 * q : 4 * q + 4, :].bitcast(I32))
         nc.sync.dma_start(n3_sb[:], n3)
@@ -82,141 +88,156 @@ def tile_picked_toketwghard_none_po_kernel(
         xgs = sb([P, PACK, P], U8, "xgs")
         xgw = sb([P, PACK, P], U32, "xgw")
         nc.vector.tensor_copy(xgs[:].rearrange("p t m -> p m t"), xs[:].indirect(offs_sb[:]))
-        nc.vector.tensor_copy(xgw[:].rearrange("p t m -> p m t"), xw[:].bitcast(U32).indirect(offs_sb[:]))
 
         wa_codes = sb([P, H], U32, "wa_codes")
         wa_scales = sb([P, H], U8, "wa_scales")
-        for a, (c0, w) in enumerate(WA_PIECES):
+
+        def quantise_wa(a):
+            c0, w = WA_PIECES[a]
             wa_bf = sb([P, w, PACK], BF16, "wa_bf%d" % a)
-            if a == 0:
-                nc.scalar.activation(weave_out(wa_bf[:]), weave_in(wa_raw[a][:]), ACT.Copy)
-            else:
-                nc.vector.tensor_copy(weave_out(wa_bf[:]), weave_in(wa_raw[a][:]))
+            nc.scalar.activation(weave_out(wa_bf[:]), weave_in(wa_raw[a][:]), ACT.Copy)
             nc.vector.quantize_mx(
                 out=wa_codes[:, c0 : c0 + w].bitcast(FP8X4), scales=wa_scales[:, c0 : c0 + w], in_=wa_bf[:].rearrange("p w t -> p (w t)")
             )
 
-        y = [sb([P, H], F32, "y%d" % t) for t in range(PACK)]
-        top = [sb([P, 2], F32, "top%d" % t) for t in range(PACK)]
+        quantise_wa(0)
+        nc.vector.tensor_copy(xgw[:].rearrange("p t m -> p m t"), xw[:].bitcast(U32).indirect(offs_sb[:]))
+        quantise_wa(1)
+        quantise_wa(2)
+
+        y = [sb([P, 2 * H if t == 0 else H], F32, "y%d" % t) for t in range(PACK)]
+        nc.vector.memset(y[0][:, H:], 0.0)
+        top = [sb([P, 1], F32, "top%d" % t) for t in range(PACK)]
         bias = [sb([P, 2], F32, "bias%d" % t) for t in range(PACK)]
-        y_ps = {}
-        for half in range(2):
-            cols = slice(half * HALF, (half + 1) * HALF)
-            for t in range(PACK):
-                bank = psum.tile([P, H], F32, name="y_ps%d_%d" % (half, t), tag="bank%d_%d" % (half, t))
-                y_ps[half, t] = bank
-                nc.tensor.matmul_mx(
-                    out=bank[:, :HALF], lhsT=xgw[:, t, :].bitcast(FP8X4), lhsT_scale=xgs[:, t, :],
-                    rhs=wa_codes[:, cols].bitcast(FP8X4), rhs_scale=wa_scales[:, cols], start=True, stop=True,
-                )
         for t in range(PACK):
-            nc.vector.tensor_scalar(y[t][:, :HALF], y_ps[0, t][:, :HALF], 1.0, None, ALU.mult, ALU.max, accum_out=top[t][:, 0:1])
-            nc.vector.tensor_scalar(y[t][:, HALF:], y_ps[1, t][:, :HALF], 1.0, top[t][:, 0:1], ALU.mult, ALU.max, accum_out=top[t][:, 1:2])
-            nc.vector.tensor_scalar(bias[t][:], rates[:, 0:2, t], top[t][:, 1:2], -1.0, ALU.mult, ALU.mult)
+            bank = psum.tile([P, H], F32, name="y_ps%d" % t, tag="bank1_%d" % t)
+            nc.tensor.matmul_mx(
+                out=bank[:], lhsT=xgw[:, t, :].bitcast(FP8X4), lhsT_scale=xgs[:, t, :],
+                rhs=wa_codes[:].bitcast(FP8X4), rhs_scale=wa_scales[:], start=True, stop=True,
+            )
+            nc.vector.tensor_scalar(y[t][:, :H], bank[:], 1.0, None, ALU.mult, ALU.max, accum_out=top[t][:])
+            nc.gpsimd.tensor_scalar(bias[t][:], rates[:, 0:2, t], top[t][:], -1.0, ALU.mult, ALU.mult)
 
         gain = sb([P, PACK], F32, "gain")
-        nc.vector.tensor_scalar(gain[:], rates[:, 2, 0:PACK], 3.0, None, ALU.mult)
+        nc.gpsimd.tensor_scalar(gain[:], rates[:, 2, 0:PACK], 3.0, 0.0, ALU.mult, ALU.add)
 
-        w1w_d = sb([P, PACK, P], U32, "w1w_d")
-        w1s_d = sb([P, PACK, P], U8, "w1s_d")
-        nc.scalar.copy(w1w_d[:], w1w[:].bitcast(U32).rearrange("p (m t) -> p t m", t=PACK))
-        nc.vector.tensor_copy(w1s_d[:].rearrange("p t m -> p m t"), w1s[:].rearrange("p (m t) -> p m t", t=PACK))
+        w1w_d = sb([P, PACK, P], I32, "w1w_d", tag="wa_codes")
+        w1s_d = sb([P, PACK, P], U8, "w1s_d", tag="wa_scales")
 
-        ea_ring = [sb([P, HALF], F32, "ea%d" % i) for i in range(RING)]
-        eb_ring = [sb([P, HALF], F32, "eb%d" % i) for i in range(RING)]
-        early = H - Z_CHUNKS[-1][1]
-        h_early = [psum.tile([P, H], F32, name="h_early%d" % t, tag="bank0_%d" % t) for t in range(PACK)]
-        h_last = []
-        for c, (c0, w) in enumerate(Z_CHUNKS):
-            entries = slice(c0 // LIST_ROWS, (c0 + w) // LIST_ROWS)
-            diff = sb([P, PACK, w], F32, "diff%d" % c)
-            for t in range(PACK):
-                ea = ea_ring[(c * PACK + t) % RING][:, :w]
-                eb = eb_ring[(c * PACK + t) % RING][:, :w]
-                ebg = sb([P, w], F32, "ebg%d_%d" % (c, t))
-                nc.scalar.activation(eb, y[t][:].indirect(n2_sb[:, entries]), ACT.Exp, bias=bias[t][:, 1:2], scale=rates[:, 1, t : t + 1])
-                nc.scalar.activation(ea, y[t][:].indirect(n1_sb[:, entries]), ACT.Exp, bias=bias[t][:, 0:1], scale=rates[:, 0, t : t + 1])
-                nc.vector.tensor_scalar(ebg[:], eb, gain[:, t : t + 1], None, ALU.mult)
-                nc.vector.scalar_tensor_tensor(diff[:, t, :], ea, gain[:, t : t + 1], ebg[:], ALU.mult, ALU.subtract)
-            z_bf = sb([P, w, PACK], BF16, "z_bf%d" % c)
-            nc.vector.tensor_copy(weave_out(z_bf[:]), weave_in(diff[:]))
+        def deal_w1():
+            nc.vector.tensor_copy(w1w_d[:].rearrange("p t m -> p m t"), w1w[:].rearrange("p (m t) -> p m t", t=PACK))
+            nc.vector.tensor_copy(w1s_d[:].rearrange("p t m -> p m t"), w1s[:].rearrange("p (m t) -> p m t", t=PACK))
+
+        z32 = [sb([P, PACK, w], F32, "z32_%d" % c) for c, (c0, w) in enumerate(Z_CHUNKS)]
+        h_ps = [[psum.tile([P, H], F32, name="h_ps%d_%d" % (half, t), tag="bank%d_%d" % (half, t)) for t in range(PACK)] for half in range(2)]
+        ea_buf = [sb([P, H], F32, "ea_buf%d" % i) for i in range(2)]
+        eb_buf = [sb([P, H], F32, "eb_buf%d" % i) for i in range(2)]
+        z_bf = {}
+
+        def round_z(c):
+            z_bf[c] = sb([P, Z_CHUNKS[c][1], PACK], BF16, "z_bf%d" % c)
+            nc.vector.tensor_copy(weave_out(z_bf[c][:]), weave_in(z32[c][:]))
+
+        def second_product(c):
+            c0, w = Z_CHUNKS[c]
             z_codes = sb([P, w], U32, "z_codes%d" % c)
             z_scales = sb([P, w], U8, "z_scales%d" % c)
-            nc.vector.quantize_mx(out=z_codes[:].bitcast(FP8X4), scales=z_scales[:], in_=z_bf[:].rearrange("p w t -> p (w t)"))
+            nc.vector.quantize_mx(out=z_codes[:].bitcast(FP8X4), scales=z_scales[:], in_=z_bf[c][:].rearrange("p w t -> p (w t)"))
             for t in range(PACK):
-                if c0 < early:
-                    h_ps = h_early[t][:, c0 : c0 + w]
-                else:
-                    bank = psum.tile([P, H], F32, name="h_last%d" % t, tag="bank1_%d" % t)
-                    h_ps = bank[:, :w]
-                    h_last.append(h_ps)
                 nc.tensor.matmul_mx(
-                    out=h_ps, lhsT=w1w_d[:, t, :].bitcast(FP8X4), lhsT_scale=w1s_d[:, t, :],
+                    out=h_ps[c0 // HALF][t][:, c0 % HALF : c0 % HALF + w], lhsT=w1w_d[:, t, :].bitcast(FP8X4), lhsT_scale=w1s_d[:, t, :],
                     rhs=z_codes[:].bitcast(FP8X4), rhs_scale=z_scales[:], start=True, stop=True,
                 )
 
-        for t in range(PACK):
-            nc.scalar.activation(hh[t][:, :early], h_early[t][:, :early], ACT.Copy, scale=0.5)
-        for t in range(PACK):
-            if t % 2 == 0:
-                nc.vector.tensor_scalar(hh[t][:, early:H], h_last[t], 0.5, None, ALU.mult)
-            else:
-                nc.scalar.activation(hh[t][:, early:H], h_last[t], ACT.Copy, scale=0.5)
+        rounded = []
+        for i, (t, e0, n) in enumerate(EXP_STEPS):
+            entries = slice(e0 // LIST_ROWS, (e0 + n) // LIST_ROWS)
+            ea = ea_buf[i % 2][:, :n]
+            eb = eb_buf[i % 2][:, :n]
+            ebg = sb([P, n], F32, "ebg%d" % i, tag={1: "w1w", 2: "w1s"}.get(i, ""))
+            nc.scalar.activation(eb, y[t][:].indirect(n2_sb[:, entries]), ACT.Exp, bias=bias[t][:, 1:2], scale=rates[:, 1, t : t + 1])
+            nc.scalar.activation(ea, y[t][:].indirect(n1_sb[:, entries]), ACT.Exp, bias=bias[t][:, 0:1], scale=rates[:, 0, t : t + 1])
+            nc.vector.tensor_scalar(ebg[:], eb, gain[:, t : t + 1], None, ALU.mult)
+            complete = []
+            for c, (c0, w) in enumerate(Z_CHUNKS):
+                if e0 <= c0 < e0 + n:
+                    cols = slice(c0 - e0, c0 - e0 + w)
+                    nc.vector.scalar_tensor_tensor(z32[c][:, t, :], ea[:, cols], gain[:, t : t + 1], ebg[:, cols], ALU.mult, ALU.subtract)
+                    if t == PACK - 1:
+                        complete.append(c)
+            if i == 0:
+                deal_w1()
+            for c in rounded:
+                second_product(c)
+            for c in complete:
+                round_z(c)
+            rounded = complete
+        for c in rounded:
+            second_product(c)
 
+        for t in range(PACK):
+            nc.scalar.activation(hh[t][:, :HALF], h_ps[0][t][:, :HALF], ACT.Copy, scale=0.5)
         out_rows = out_0.rearrange("(p t) j -> p t j", t=PACK)
         out_words = out_1[0].rearrange("p n t -> p (n t)").bitcast(I32)
         o_codes = sb([P, H], U32, "o_codes")
         o_scales = sb([P, H], U8, "o_scales")
         res = [sb([P, PACK, w], F32, "o%d" % c) for c, (c0, w) in enumerate(OUT_CHUNKS)]
-        units = [(c, t) for c in range(len(OUT_CHUNKS)) for t in range(PACK)]
+        wide = OUT_CHUNKS[0][1]
+        units = [(0, t, 1) for t in range(PACK)] + [(1, t, 2) for t in range(0, PACK, 2)]
         held = {}
-        pair_ring = [sb([P, HALF, 2], F32, "pair%d" % i) for i in range(RING)]
+        pair_ring = [sb([P, wide, 2], F32, "pair%d" % i) for i in range(RING)]
 
         def front(u):
-            c, t = units[u]
+            c, t0, tiles = units[u]
             c0, w = OUT_CHUNKS[c]
-            entries = slice(2 * c0 // LIST_ROWS, 2 * (c0 + w) // LIST_ROWS)
-            pair = pair_ring[u % RING][:, :w, :]
-            picked = hh[t][:].indirect(n3_sb[:, entries])
-            flat = pair.rearrange("p j e -> p (j e)")
-            if u == 0:
-                nc.vector.tensor_copy(flat, picked)
-            else:
-                nc.scalar.activation(flat, picked, ACT.Copy)
-            big = sb([P, w], F32, "big%d" % u)
-            small = sb([P, w], F32, "small%d" % u)
-            th = sb([P, w], F32, "th%d" % u)
+            entries = n3_sb[:, 2 * c0 // LIST_ROWS : 2 * (c0 + w) // LIST_ROWS]
+            pair = pair_ring[u % RING][:, : tiles * w, :]
+            for i in range(tiles):
+                t = t0 + i
+                flat = pair[:, i * w : (i + 1) * w, :].rearrange("p j e -> p (j e)")
+                if u == 0:
+                    nc.vector.tensor_scalar(hh[t][:, HALF:H], h_ps[1][t][:, :HALF], 0.5, None, ALU.mult)
+                    nc.vector.tensor_copy(flat, hh[t][:].indirect(entries))
+                else:
+                    if c == 0:
+                        nc.scalar.activation(hh[t][:, HALF:H], h_ps[1][t][:, :HALF], ACT.Copy, scale=0.5)
+                    nc.scalar.activation(flat, hh[t][:].indirect(entries), ACT.Copy)
+            big = sb([P, tiles * w], F32, "big%d" % u)
+            small = sb([P, tiles * w], F32, "small%d" % u)
+            th = sb([P, tiles * w], F32, "th%d" % u)
             nc.vector.tensor_tensor(big[:], pair[:, :, 0], pair[:, :, 1], ALU.max)
             nc.vector.tensor_tensor(small[:], pair[:, :, 0], pair[:, :, 1], ALU.min)
             nc.scalar.activation(th[:], big[:], ACT.Tanh)
             held[u] = (small, th)
 
         def middle(u):
-            c, t = units[u]
+            c, t0, tiles = units[u]
             c0, w = OUT_CHUNKS[c]
             small, th = held[u]
-            rest = sb([P, w], F32, "rest%d" % u)
-            nc.vector.tensor_tensor(rest[:], hh[t][:, c0 : c0 + w], small[:], ALU.subtract)
+            rest = sb([P, tiles * w], F32, "rest%d" % u)
+            for i in range(tiles):
+                cols = slice(i * w, (i + 1) * w)
+                nc.vector.tensor_tensor(rest[:, cols], hh[t0 + i][:, c0 : c0 + w], small[:, cols], ALU.subtract)
             held[u] = (rest, th)
 
         def back(u):
-            c, t = units[u]
+            c, t0, tiles = units[u]
             c0, w = OUT_CHUNKS[c]
             rest, th = held[u]
-            nc.vector.scalar_tensor_tensor(res[c][:, t, :], th[:], 1.0, rest[:], ALU.add, ALU.mult)
-            if t == PACK - 1:
+            rows = res[c][:, t0 : t0 + tiles, :].rearrange("p t j -> p (t j)")
+            nc.vector.scalar_tensor_tensor(rows, th[:], 1.0, rest[:], ALU.add, ALU.mult)
+            if t0 + tiles == PACK:
                 nc.sync.dma_start(out_rows[:, :, c0 : c0 + w], res[c][:])
 
-        def planes(c):
-            c0, w = OUT_CHUNKS[c]
-            o_bf = sb([P, w, PACK], BF16, "o_bf%d" % c)
-            if c < len(OUT_CHUNKS) - 1:
-                nc.scalar.activation(weave_out(o_bf[:]), weave_in(res[c][:]), ACT.Copy)
+        def planes(c, j0, j1):
+            c0 = OUT_CHUNKS[c][0]
+            o_bf = sb([P, j1 - j0, PACK], BF16, "o_bf%d_%d" % (c, j0))
+            if c == 0:
+                nc.scalar.activation(weave_out(o_bf[:]), weave_in(res[c][:, :, j0:j1]), ACT.Copy)
             else:
-                nc.vector.tensor_copy(weave_out(o_bf[:]), weave_in(res[c][:]))
-            cols = slice(c0, c0 + w)
+                nc.vector.tensor_copy(weave_out(o_bf[:]), weave_in(res[c][:, :, j0:j1]))
+            cols = slice(c0 + j0, c0 + j1)
             nc.vector.quantize_mx(out=o_codes[:, cols].bitcast(FP8X4), scales=o_scales[:, cols], in_=o_bf[:].rearrange("p w t -> p (w t)"))
-            nc.sync.dma_start(out_words[:, cols], o_codes[:, cols].bitcast(I32))
 
         for u in range(len(units)):
             front(u)
@@ -224,8 +245,11 @@ def tile_picked_toketwghard_none_po_kernel(
                 back(u - 1)
             middle(u)
         back(len(units) - 1)
-        for c in range(len(OUT_CHUNKS)):
-            planes(c)
+        planes(0, 0, HALF)
+        nc.sync.dma_start(out_words[:, :HALF], o_codes[:, :HALF].bitcast(I32))
+        planes(0, HALF, wide)
+        planes(1, 0, H - wide)
+        nc.sync.dma_start(out_words[:, HALF:], o_codes[:, HALF:].bitcast(I32))
         for q in range(4):
             eng = nc.scalar if q % 2 == 0 else nc.sync
             eng.dma_start(out_2[0][4 * q : 4 * q + 4, :].bitcast(I32), o_scales[32 * q : 32 * q + 4, :].bitcast(I32))

@@ -187,21 +187,29 @@ def tile_picked_toketwghard_none_po_kernel(
         held = {}
         pair_ring = [sb([P, wide, 2], F32, "pair%d" % i) for i in range(RING)]
 
+        def fetch(u, i, on_vector):
+            c, t0, tiles = units[u]
+            c0, w = OUT_CHUNKS[c]
+            picked = hh[t0 + i][:].indirect(n3_sb[:, 2 * c0 // LIST_ROWS : 2 * (c0 + w) // LIST_ROWS])
+            flat = pair_ring[u % RING][:, i * w : (i + 1) * w, :].rearrange("p j e -> p (j e)")
+            if on_vector:
+                nc.vector.tensor_copy(flat, picked)
+            else:
+                nc.scalar.activation(flat, picked, ACT.Copy)
+
         def front(u):
             c, t0, tiles = units[u]
             c0, w = OUT_CHUNKS[c]
-            entries = n3_sb[:, 2 * c0 // LIST_ROWS : 2 * (c0 + w) // LIST_ROWS]
             pair = pair_ring[u % RING][:, : tiles * w, :]
+            if u == 0:
+                nc.vector.tensor_scalar(hh[t0][:, HALF:H], h_ps[1][t0][:, :HALF], 0.5, None, ALU.mult)
+            elif c == 0:
+                nc.scalar.activation(hh[t0][:, HALF:H], h_ps[1][t0][:, :HALF], ACT.Copy, scale=0.5)
+            if u == PACK - 1:
+                fetch(PACK, 0, True)
             for i in range(tiles):
-                t = t0 + i
-                flat = pair[:, i * w : (i + 1) * w, :].rearrange("p j e -> p (j e)")
-                if u == 0:
-                    nc.vector.tensor_scalar(hh[t][:, HALF:H], h_ps[1][t][:, :HALF], 0.5, None, ALU.mult)
-                    nc.vector.tensor_copy(flat, hh[t][:].indirect(entries))
-                else:
-                    if c == 0:
-                        nc.scalar.activation(hh[t][:, HALF:H], h_ps[1][t][:, :HALF], ACT.Copy, scale=0.5)
-                    nc.scalar.activation(flat, hh[t][:].indirect(entries), ACT.Copy)
+                if (u, i) != (PACK, 0):
+                    fetch(u, i, u == 0)
             big = sb([P, tiles * w], F32, "big%d" % u)
             small = sb([P, tiles * w], F32, "small%d" % u)
             th = sb([P, tiles * w], F32, "th%d" % u)

from contextlib import ExitStack

import concourse.mybir as mybir

K, T, S, N, H = 512, 2048, 512, 512, 512
FLOPS = 2 * K * S * H + 2 * S * N * H

F32 = mybir.dt.float32
BF16 = mybir.dt.bfloat16
I32 = mybir.dt.int32
U32 = mybir.dt.uint32
U16 = mybir.dt.uint16
U8 = mybir.dt.uint8
FP8X4 = mybir.dt.float8_e4m3fn_x4
ALU = mybir.AluOpType
ACT = mybir.ActivationFunctionType

P = 128
PACK = 4
LIST_ROWS = 16
SPARE = 272
WA_PIECES = [(0, 256), (256, 128), (384, 128)]
HALF = H // 2
RING = 2
Z_CHUNKS = [(0, 256), (256, 128), (384, 128)]
OUT_CHUNKS = [(0, 384), (384, 128)]
EXP_STEPS = [(0, 0, 512), (1, 0, 256), (2, 0, 256), (3, 0, 256), (1, 256, 256), (2, 256, 256), (3, 256, 128), (3, 384, 128)]


def weave_out(grouped):
    return grouped.rearrange("p (c i) t -> p c t i", i=4)


def weave_in(rows):
    return rows.rearrange("p t (c i) -> p c t i", i=4)


def tile_picked_toketwghard_none_po_kernel(
    tc, x_words, x_scales, wa, tau, tau2, gt, w1_words, w1_scales, offs, n1, n2, n3, out_0, out_1, out_2
):
    nc = tc.nc
    with ExitStack() as ctx:
        keep = ctx.enter_context(tc.tile_pool(name="keep", bufs=1))
        psum = ctx.enter_context(tc.psum_pool(name="psum", bufs=1))

        def sb(shape, dtype, name, tag=""):
            return keep.tile(shape, dtype, name=name, tag=tag or name, align_bytes=64)

        offs_sb = sb([P, S // LIST_ROWS], U16, "offs_sb")
        n1_sb = sb([P, H // LIST_ROWS], U16, "n1_sb")
        n2_sb = sb([P, H // LIST_ROWS], U16, "n2_sb")
        n3_sb = sb([P, 2 * H // LIST_ROWS], U16, "n3_sb")

        xw = sb([P, T], I32, "xw")
        xs = sb([P, T], U8, "xs")
        w1w = sb([P, N], I32, "w1w")
        w1s = sb([P, N], U8, "w1s")
        wa_raw = [sb([P, PACK, w], F32, "wa_raw%d" % a) for a, (c0, w) in enumerate(WA_PIECES)]
        rates = sb([P, 3, 8], F32, "rates")
        hh = [sb([P, H + SPARE], F32, "hh%d" % t) for t in range(PACK)]

        nc.vector.memset(xs[:].bitcast(I32), 0)
        wa_rows = wa.rearrange("(p j) h -> p j h", j=PACK)

        def load_wa(a):
            c0, w = WA_PIECES[a]
            nc.sync.dma_start(wa_raw[a][:], wa_rows[:, :, c0 : c0 + w])

        nc.sync.dma_start(offs_sb[:], offs)
        load_wa(0)
        for q in range(4):
            nc.sync.dma_start(xs[32 * q : 32 * q + 4, :].bitcast(I32), x_scales[0][4 * q : 4 * q + 4, :].bitcast(I32))
        nc.sync.dma_start(xw[:], x_words[0].rearrange("p n t -> p (n t)").bitcast(I32))
        load_wa(1)
        load_wa(2)
        nc.vector.memset(w1s[:].bitcast(I32), 0)
        for t in range(PACK):
            nc.vector.memset(hh[t][:, H:], 0.0)
        nc.sync.dma_start(n2_sb[:], n2)
        nc.sync.dma_start(n1_sb[:], n1)
        for r, vec in enumerate((tau, tau2, gt)):
            nc.gpsimd.dma_start(rates[:, r, 0:PACK], vec.rearrange("(p t) o -> p (t o)", t=PACK))
        nc.sync.dma_start(w1w[:], w1_words[0].rearrange("p n t -> p (n t)").bitcast(I32))
        for q in range(4):
            nc.sync.dma_start(w1s[32 * q : 32 * q + 4, :].bitcast(I32), w1_scales[0][4 * q : 4 * q + 4, :].bitcast(I32))
        nc.sync.dma_start(n3_sb[:], n3)

        xgs = sb([P, PACK, P], U8, "xgs")
        xgw = sb([P, PACK, P], U32, "xgw")
        nc.vector.tensor_copy(xgs[:].rearrange("p t m -> p m t"), xs[:].indirect(offs_sb[:]))

        wa_codes = sb([P, H], U32, "wa_codes")
        wa_scales = sb([P, H], U8, "wa_scales")

        def quantise_wa(a):
            c0, w = WA_PIECES[a]
            wa_bf = sb([P, w, PACK], BF16, "wa_bf%d" % a)
            nc.scalar.activation(weave_out(wa_bf[:]), weave_in(wa_raw[a][:]), ACT.Copy)
            nc.vector.quantize_mx(
                out=wa_codes[:, c0 : c0 + w].bitcast(FP8X4), scales=wa_scales[:, c0 : c0 + w], in_=wa_bf[:].rearrange("p w t -> p (w t)")
            )

        quantise_wa(0)
        nc.vector.tensor_copy(xgw[:].rearrange("p t m -> p m t"), xw[:].bitcast(U32).indirect(offs_sb[:]))
        quantise_wa(1)
        quantise_wa(2)

        y = [sb([P, 2 * H if t == 0 else H], F32, "y%d" % t) for t in range(PACK)]
        nc.vector.memset(y[0][:, H:], 0.0)
        top = [sb([P, 1], F32, "top%d" % t) for t in range(PACK)]
        bias = [sb([P, 2], F32, "bias%d" % t) for t in range(PACK)]
        for t in range(PACK):
            bank = psum.tile([P, H], F32, name="y_ps%d" % t, tag="bank1_%d" % t)
            nc.tensor.matmul_mx(
                out=bank[:], lhsT=xgw[:, t, :].bitcast(FP8X4), lhsT_scale=xgs[:, t, :],
                rhs=wa_codes[:].bitcast(FP8X4), rhs_scale=wa_scales[:], start=True, stop=True,
            )
            nc.vector.tensor_scalar(y[t][:, :H], bank[:], 1.0, None, ALU.mult, ALU.max, accum_out=top[t][:])
            nc.gpsimd.tensor_scalar(bias[t][:], rates[:, 0:2, t], top[t][:], -1.0, ALU.mult, ALU.mult)

        gain = sb([P, PACK], F32, "gain")
        nc.gpsimd.tensor_scalar(gain[:], rates[:, 2, 0:PACK], 3.0, 0.0, ALU.mult, ALU.add)

        w1w_d = sb([P, PACK, P], I32, "w1w_d", tag="wa_codes")
        w1s_d = sb([P, PACK, P], U8, "w1s_d", tag="wa_scales")

        def deal_w1():
            nc.vector.tensor_copy(w1w_d[:].rearrange("p t m -> p m t"), w1w[:].rearrange("p (m t) -> p m t", t=PACK))
            nc.vector.tensor_copy(w1s_d[:].rearrange("p t m -> p m t"), w1s[:].rearrange("p (m t) -> p m t", t=PACK))

        z32 = [sb([P, PACK, w], F32, "z32_%d" % c) for c, (c0, w) in enumerate(Z_CHUNKS)]
        h_ps = [[psum.tile([P, H], F32, name="h_ps%d_%d" % (half, t), tag="bank%d_%d" % (half, t)) for t in range(PACK)] for half in range(2)]
        ea_buf = [sb([P, H], F32, "ea_buf%d" % i) for i in range(2)]
        eb_buf = [sb([P, H], F32, "eb_buf%d" % i) for i in range(2)]
        z_bf = {}

        def round_z(c):
            z_bf[c] = sb([P, Z_CHUNKS[c][1], PACK], BF16, "z_bf%d" % c)
            nc.vector.tensor_copy(weave_out(z_bf[c][:]), weave_in(z32[c][:]))

        def second_product(c):
            c0, w = Z_CHUNKS[c]
            z_codes = sb([P, w], U32, "z_codes%d" % c)
            z_scales = sb([P, w], U8, "z_scales%d" % c)
            nc.vector.quantize_mx(out=z_codes[:].bitcast(FP8X4), scales=z_scales[:], in_=z_bf[c][:].rearrange("p w t -> p (w t)"))
            for t in range(PACK):
                nc.tensor.matmul_mx(
                    out=h_ps[c0 // HALF][t][:, c0 % HALF : c0 % HALF + w], lhsT=w1w_d[:, t, :].bitcast(FP8X4), lhsT_scale=w1s_d[:, t, :],
                    rhs=z_codes[:].bitcast(FP8X4), rhs_scale=z_scales[:], start=True, stop=True,
                )

        rounded = []
        for i, (t, e0, n) in enumerate(EXP_STEPS):
            entries = slice(e0 // LIST_ROWS, (e0 + n) // LIST_ROWS)
            ea = ea_buf[i % 2][:, :n]
            eb = eb_buf[i % 2][:, :n]
            ebg = sb([P, n], F32, "ebg%d" % i, tag={1: "w1w", 2: "w1s"}.get(i, ""))
            nc.scalar.activation(eb, y[t][:].indirect(n2_sb[:, entries]), ACT.Exp, bias=bias[t][:, 1:2], scale=rates[:, 1, t : t + 1])
            nc.scalar.activation(ea, y[t][:].indirect(n1_sb[:, entries]), ACT.Exp, bias=bias[t][:, 0:1], scale=rates[:, 0, t : t + 1])
            nc.vector.tensor_scalar(ebg[:], eb, gain[:, t : t + 1], None, ALU.mult)
            complete = []
            for c, (c0, w) in enumerate(Z_CHUNKS):
                if e0 <= c0 < e0 + n:
                    cols = slice(c0 - e0, c0 - e0 + w)
                    nc.vector.scalar_tensor_tensor(z32[c][:, t, :], ea[:, cols], gain[:, t : t + 1], ebg[:, cols], ALU.mult, ALU.subtract)
                    if t == PACK - 1:
                        complete.append(c)
            if i == 0:
                deal_w1()
            for c in rounded:
                second_product(c)
            for c in complete:
                round_z(c)
            rounded = complete
        for c in rounded:
            second_product(c)

        for t in range(PACK):
            nc.scalar.activation(hh[t][:, :HALF], h_ps[0][t][:, :HALF], ACT.Copy, scale=0.5)
        out_rows = out_0.rearrange("(p t) j -> p t j", t=PACK)
        out_words = out_1[0].rearrange("p n t -> p (n t)").bitcast(I32)
        o_codes = sb([P, H], U32, "o_codes")
        o_scales = sb([P, H], U8, "o_scales")
        res = [sb([P, PACK, w], F32, "o%d" % c) for c, (c0, w) in enumerate(OUT_CHUNKS)]
        wide = OUT_CHUNKS[0][1]
        units = [(0, t, 1) for t in range(PACK)] + [(1, t, 2) for t in range(0, PACK, 2)]
        held = {}
        pair_ring = [sb([P, wide, 2], F32, "pair%d" % i) for i in range(RING)]

        def fetch(u, i, on_vector):
            c, t0, tiles = units[u]
            c0, w = OUT_CHUNKS[c]
            picked = hh[t0 + i][:].indirect(n3_sb[:, 2 * c0 // LIST_ROWS : 2 * (c0 + w) // LIST_ROWS])
            flat = pair_ring[u % RING][:, i * w : (i + 1) * w, :].rearrange("p j e -> p (j e)")
            if on_vector:
                nc.vector.tensor_copy(flat, picked)
            else:
                nc.scalar.activation(flat, picked, ACT.Copy)

        def front(u):
            c, t0, tiles = units[u]
            c0, w = OUT_CHUNKS[c]
            pair = pair_ring[u % RING][:, : tiles * w, :]
            if u == 0:
                nc.vector.tensor_scalar(hh[t0][:, HALF:H], h_ps[1][t0][:, :HALF], 0.5, None, ALU.mult)
            elif c == 0:
                nc.scalar.activation(hh[t0][:, HALF:H], h_ps[1][t0][:, :HALF], ACT.Copy, scale=0.5)
            if u == PACK - 1:
                fetch(PACK, 0, True)
            for i in range(tiles):
                if (u, i) != (PACK, 0):
                    fetch(u, i, u == 0)
            big = sb([P, tiles * w], F32, "big%d" % u)
            small = sb([P, tiles * w], F32, "small%d" % u)
            th = sb([P, tiles * w], F32, "th%d" % u)
            nc.vector.tensor_tensor(big[:], pair[:, :, 0], pair[:, :, 1], ALU.max)
            nc.vector.tensor_tensor(small[:], pair[:, :, 0], pair[:, :, 1], ALU.min)
            nc.scalar.activation(th[:], big[:], ACT.Tanh)
            held[u] = (small, th)

        def middle(u):
            c, t0, tiles = units[u]
            c0, w = OUT_CHUNKS[c]
            small, th = held[u]
            rest = sb([P, tiles * w], F32, "rest%d" % u)
            for i in range(tiles):
                cols = slice(i * w, (i + 1) * w)
                nc.vector.tensor_tensor(rest[:, cols], hh[t0 + i][:, c0 : c0 + w], small[:, cols], ALU.subtract)
            held[u] = (rest, th)

        def back(u):
            c, t0, tiles = units[u]
            c0, w = OUT_CHUNKS[c]
            rest, th = held[u]
            rows = res[c][:, t0 : t0 + tiles, :].rearrange("p t j -> p (t j)")
            nc.vector.scalar_tensor_tensor(rows, th[:], 1.0, rest[:], ALU.add, ALU.mult)
            if t0 + tiles == PACK:
                nc.sync.dma_start(out_rows[:, :, c0 : c0 + w], res[c][:])

        def planes(c, j0, j1):
            c0 = OUT_CHUNKS[c][0]
            o_bf = sb([P, j1 - j0, PACK], BF16, "o_bf%d_%d" % (c, j0))
            if c == 0:
                nc.scalar.activation(weave_out(o_bf[:]), weave_in(res[c][:, :, j0:j1]), ACT.Copy)
            else:
                nc.vector.tensor_copy(weave_out(o_bf[:]), weave_in(res[c][:, :, j0:j1]))
            cols = slice(c0 + j0, c0 + j1)
            nc.vector.quantize_mx(out=o_codes[:, cols].bitcast(FP8X4), scales=o_scales[:, cols], in_=o_bf[:].rearrange("p w t -> p (w t)"))

        for u in range(len(units)):
            front(u)
            if u > 0:
                back(u - 1)
            middle(u)
        back(len(units) - 1)
        planes(0, 0, HALF)
        nc.sync.dma_start(out_words[:, :HALF], o_codes[:, :HALF].bitcast(I32))
        planes(0, HALF, wide)
        planes(1, 0, H - wide)
        nc.sync.dma_start(out_words[:, HALF:], o_codes[:, HALF:].bitcast(I32))
        for q in range(4):
            eng = nc.scalar if q % 2 == 0 else nc.sync
            eng.dma_start(out_2[0][4 * q : 4 * q + 4, :].bitcast(I32), o_scales[32 * q : 32 * q + 4, :].bitcast(I32))
